import numpy as np
import ml_dtypes


def mxq(x, axis, fmt="e4m3"):
    dtype, down = {"e4m3": (ml_dtypes.float8_e4m3fn, 7), "e5m2": (ml_dtypes.float8_e5m2, 14)}[fmt]
    v = np.moveaxis(np.asarray(x, np.float32).astype(ml_dtypes.bfloat16).astype(np.float64), axis, -1)
    blocks = v.reshape(v.shape[:-1] + (-1, 32))
    amax = np.abs(blocks).max(-1, keepdims=True)
    byte = np.maximum(np.where(amax > 0, np.frexp(amax)[1] - 1 + 127, 0) - down, 1)
    scale = np.exp2(byte - 127.0)
    codes = (blocks / scale).astype(np.float32).astype(dtype).astype(np.float64)
    return np.moveaxis((codes * scale).reshape(v.shape), -1, axis)


WIDE = False


def mx_kscale(k):
    if not WIDE:
        return np.ones(k)
    levels = np.array([10, -10, 5, -5, 0])
    if k % 512:
        return np.exp2(np.random.permutation(np.resize(levels, k // 32))).repeat(32)
    a = np.empty((k // 512, 16))
    for p in range(k // 512):
        a[p, :8] = np.random.permutation(np.resize(levels, 8))
        for g in range(8):
            far = levels[np.abs(levels - a[p, g]) >= 10]
            a[p, g + 8] = far[np.random.randint(len(far))]
    return np.exp2(a.ravel()).repeat(32)


def f64(x):
    return np.asarray(x).astype(np.float64)


def striped(idx):
    return np.tile(idx.reshape(-1, 16).T, (8, 1)).astype(np.uint16)


def unstriped(offs):
    return offs[:16].T.reshape(-1).astype(np.int64)


def striped8(idx):
    return np.concatenate([x.reshape(-1, 16).T for x in idx]).astype(np.uint16)


def runs(offs, k):
    lists = np.stack([offs[16 * r : 16 * r + 16].T.reshape(-1) for r in range(8)]).astype(np.int64)
    return lists[np.arange(k) % 512 // 64]


def pack_weight(w):
    k, n = w.shape
    w = f64(np.asarray(w, np.float32).astype(ml_dtypes.bfloat16)).reshape(k // 32, 32, n)
    amax = np.abs(w).max(1)
    byte = np.clip(np.where(amax > 0, np.frexp(amax)[1] - 1 + 127 - 7, 1), 1, 254)
    scaled = (w * np.exp2(127.0 - byte)[:, None, :]).reshape(k, n).astype(np.float32)
    words = np.ascontiguousarray(scaled.reshape(k // 512, 128, 4, n).transpose(0, 1, 3, 2)).astype(ml_dtypes.float8_e4m3fn).view(np.uint8)
    return words, np.ascontiguousarray(byte.astype(np.uint8).reshape(k // 512, 16, n))


def unpack_weight(words, scales):
    g, p, n, _ = words.shape
    vals = np.ascontiguousarray(words).view(ml_dtypes.float8_e4m3fn).astype(np.float64) * np.repeat(np.exp2(scales.astype(np.float64) - 127.0), 8, axis=1)[..., None]
    return vals.transpose(0, 1, 3, 2).reshape(g * 512, n)


E2M1 = np.array([0.0, 0.5, 1.0, 1.5, 2.0, 3.0, 4.0, 6.0, -0.0, -0.5, -1.0, -1.5, -2.0, -3.0, -4.0, -6.0])


def pack_fp4(w):
    k, n = w.shape
    w = f64(np.asarray(w, np.float32).astype(ml_dtypes.bfloat16)).reshape(k // 32, 32, n)
    amax = np.abs(w).max(1)
    mant, ex = np.frexp(amax / 6.0)
    byte = np.clip(np.where(amax > 0, np.where(mant > 0.5, ex, ex - 1) + 127, 1), 1, 254)
    scaled = (w * np.exp2(127.0 - byte)[:, None, :]).reshape(k, n).astype(np.float32)
    c = np.ascontiguousarray(scaled.reshape(k // 512, 128, 4, n).transpose(0, 1, 3, 2)).astype(ml_dtypes.float4_e2m1fn).view(np.uint8) & 0xF
    words = (c[..., 0::2] | (c[..., 1::2] << 4)).reshape(k // 512, 128, 2 * n)
    return np.ascontiguousarray(words), np.ascontiguousarray(byte.astype(np.uint8).reshape(k // 512, 16, n))


def unpack_fp4(words, scales):
    g, _, n = scales.shape
    words = np.ascontiguousarray(words).reshape(g, 128, n, 2)
    nib = np.empty((g, 128, n, 4), np.uint8)
    nib[..., 0::2] = words & 0xF
    nib[..., 1::2] = words >> 4
    vals = E2M1[nib] * np.repeat(np.exp2(scales.astype(np.float64) - 127.0), 8, axis=1)[..., None]
    return vals.transpose(0, 1, 3, 2).reshape(g * 512, n)


K, T, S, N, H, W = 512, 2048, 256, 512, 512, 128


def setup_inputs():
    n = np.random.standard_normal
    s = mx_kscale(K)[:, None]
    u = mx_kscale(H)
    packed_xT = pack_weight(n((K, T)) * s)
    packed_w1 = pack_fp4(n((K, H)) / np.sqrt(K) / s)
    packed_w2 = pack_fp4(n((H, N)) / np.sqrt(H) / u[:, None])
    perm = np.random.permutation(S)
    return {
        "x_words": packed_xT[0],
        "x_scales": packed_xT[1],
        "w1_words": packed_w1[0],
        "w1_scales": packed_w1[1],
        "tau": np.random.uniform(0.3, 0.9, (H, 1)).astype(np.float32),
        "gn": (np.random.uniform(0.5, 1.5, (H, 1)) * u[:, None]).astype(np.float32),
        "w2_words": packed_w2[0],
        "w2_scales": packed_w2[1],
        "offs": striped8(np.random.randint(0, T, (8, S))),
        "n1": striped8(np.stack([np.random.permutation(S) for _ in range(8)])),
        "n2": striped(perm[:W]),
        "n3": striped(perm[W:]),
        "n4": striped(np.random.permutation(S)),
    }


def reference(x_words, x_scales, w1_words, w1_scales, tau, gn, w2_words, w2_scales, offs, n1, n2, n3, n4):
    xq = unpack_weight(x_words, x_scales)[np.arange(K)[:, None], runs(offs, K)]
    y = unpack_fp4(w1_words, w1_scales).T @ xq
    top = y.max(axis=1, keepdims=True)
    ea = np.exp(f64(tau) * (y[np.arange(H)[:, None], runs(n1, H)] - top))
    z = f64(gn) * (2.0 * (y * ea))
    h = unpack_fp4(w2_words, w2_scales).T @ mxq(z, 0, "e4m3")
    pa = h[:, unstriped(n2)]
    pb = h[:, unstriped(n3)]
    rb = np.minimum(pa, pb)
    ra = np.maximum(pa, pb)
    ds = np.zeros((N, S))
    ds[:, unstriped(n2)] = ra
    dt = ds.copy()
    dt[:, unstriped(n3)] = rb
    return dt - dt[:, unstriped(n4)]

@@ -1,0 +1,225 @@
+from contextlib import ExitStack
+
+import concourse.mybir as mybir
+
+K, T, S, H, N, W = 512, 2048, 256, 512, 512, 128
+FLOPS = 2 * K * H * S + 2 * H * N * S
+
+F32 = mybir.dt.float32
+BF16 = mybir.dt.bfloat16
+I32 = mybir.dt.int32
+U32 = mybir.dt.uint32
+U16 = mybir.dt.uint16
+U8 = mybir.dt.uint8
+FP8X4 = mybir.dt.float8_e4m3fn_x4
+FP4X4 = mybir.dt.float4_e2m1fn_x4
+ALU = mybir.AluOpType
+ACT = mybir.ActivationFunctionType
+
+P = 128
+PACK = 4
+QUAD = 32
+SUB = 8
+LIST_ROWS = 16
+HALF = S // 2
+SPARE = 16
+
+
+def tile_picked_hashepkordd_none_p_kernel(
+    tc, x_words, x_scales, w1_words, w1_scales, tau, gn, w2_words, w2_scales, offs, n1, n2, n3, n4, out
+):
+    nc = tc.nc
+    with ExitStack() as ctx:
+        keep = ctx.enter_context(tc.tile_pool(name="keep", bufs=1))
+        psum = ctx.enter_context(tc.psum_pool(name="psum", bufs=1))
+
+        offs_t = keep.tile([P, S // LIST_ROWS], U16, name="offs_t")
+        n1_t = keep.tile([P, S // LIST_ROWS], U16, name="n1_t")
+        n2_t = keep.tile([P, W // LIST_ROWS], U16, name="n2_t")
+        n3_t = keep.tile([P, W // LIST_ROWS], U16, name="n3_t")
+        n4_t = keep.tile([P, S // LIST_ROWS], U16, name="n4_t")
+
+        xw_all = keep.tile([P, T], U32, name="xw_all", align_bytes=64)
+        xs_all = keep.tile([P, T], U8, name="xs_all", align_bytes=64)
+        xw = keep.tile([P, S], U32, name="xw", align_bytes=64)
+        xs_picked = keep.tile([P, S], U8, name="xs_picked", align_bytes=64)
+        xs = keep.tile([P, S], U8, name="xs", align_bytes=64)
+        w1_raw = keep.tile([P, 2 * H], U8, name="w1_raw", align_bytes=64)
+        w1s_raw = keep.tile([P, H], U8, name="w1s_raw", align_bytes=64)
+        w1 = keep.tile([P, 2 * H], U8, name="w1", align_bytes=64)
+        w1s = keep.tile([P, H], U8, name="w1s", align_bytes=64)
+        w2 = w1_raw
+        w2s = w1s_raw
+        tau_t = keep.tile([P, PACK], F32, name="tau_t")
+        gn_t = keep.tile([P, PACK], F32, name="gn_t")
+        dt = [keep.tile([P, S + SPARE], F32, name=f"dt{m}") for m in range(N // P)]
+
+        nc.vector.memset(xs[:].bitcast(I32), 0)
+        for m in range(N // P):
+            nc.vector.memset(dt[m][:, S:], 0.0)
+
+        def load_w1_scales(queue, q):
+            queue.dma_start(
+                w1s_raw[QUAD * q : QUAD * (q + 1), :].bitcast(I32),
+                w1_scales[0, PACK * q : PACK * q + PACK, :].bitcast(I32).partition_broadcast(SUB),
+            )
+
+        nc.sync.dma_start(offs_t[:], offs)
+        nc.scalar.dma_start(
+            xs_all[:].bitcast(I32), x_scales[0].bitcast(I32).unsqueeze(1).to_broadcast([LIST_ROWS, SUB, T // 4])
+        )
+        load_w1_scales(nc.sync, 0)
+        load_w1_scales(nc.scalar, 1)
+        load_w1_scales(nc.sync, 2)
+        load_w1_scales(nc.scalar, 3)
+        nc.sync.dma_start(xw_all[:].bitcast(I32), x_words[0].rearrange("p n t -> p (n t)").bitcast(I32))
+        nc.scalar.dma_start(w1_raw[:].bitcast(I32), w1_words[0].bitcast(I32))
+        nc.sync.dma_start(n1_t[:], n1)
+        nc.gpsimd.dma_start(tau_t[:], tau.rearrange("(p t) o -> p (t o)", t=PACK))
+        nc.gpsimd.dma_start(gn_t[:], gn.rearrange("(p t) o -> p (t o)", t=PACK))
+
+        nc.vector.tensor_copy(xs_picked[:], xs_all[:].indirect(offs_t[:]))
+        for s in range(PACK):
+            nc.scalar.dma_start(xs[s:P:QUAD, :].bitcast(I32), xs_picked[SUB * s : P : QUAD, :].bitcast(I32))
+
+        nc.scalar.copy(
+            w1[:].bitcast(U16).rearrange("p (t m) -> p t m", t=PACK),
+            w1_raw[:].bitcast(U16).rearrange("p (m t) -> p t m", t=PACK),
+        )
+        nc.vector.tensor_copy(
+            w1s[:].rearrange("p (t m) -> p t m", t=PACK),
+            w1s_raw[:].rearrange("p (m t) -> p t m", t=PACK),
+        )
+        nc.vector.tensor_copy(xw[:], xw_all[:].indirect(offs_t[:]))
+
+        nc.sync.dma_start(w2[:].bitcast(I32), w2_words[0].bitcast(I32))
+        nc.sync.dma_start(n2_t[:], n2)
+        nc.sync.dma_start(n3_t[:], n3)
+        nc.sync.dma_start(n4_t[:], n4)
+        for q in range(P // QUAD):
+            nc.sync.dma_start(
+                w2s[QUAD * q : QUAD * q + PACK, :].bitcast(I32),
+                w2_scales[0, PACK * q : PACK * q + PACK, :].bitcast(I32),
+            )
+
+        last = PACK - 1
+        y = [keep.tile([P, S if t == last else 2 * S], F32, name=f"y{t}") for t in range(PACK)]
+        for t in range(last):
+            nc.vector.memset(y[t][:, S:], 0.0)
+        top = [keep.tile([P, 1], F32, name=f"top{t}") for t in range(PACK)]
+        bias = [keep.tile([P, 1], F32, name=f"bias{t}") for t in range(PACK)]
+        yg = keep.tile([P, PACK, S], F32, name="yg")
+        ea = keep.tile([P, PACK, S], F32, name="ea")
+
+        def exp_gather(t, lo, hi):
+            nc.scalar.activation(
+                out=ea[:, t, lo:hi],
+                in_=y[t][:].indirect(n1_t[:, lo // LIST_ROWS : hi // LIST_ROWS]),
+                func=ACT.Exp,
+                scale=tau_t[:, t : t + 1],
+                bias=bias[t][:],
+            )
+
+        for t in range(PACK):
+            y_ps = psum.tile([P, S], F32, name=f"y_ps{t}", tag=f"bank{t}")
+            nc.tensor.matmul_mx(
+                y_ps[:],
+                lhsT=w1[:, 2 * P * t : 2 * P * (t + 1)].bitcast(FP4X4),
+                lhsT_scale=w1s[:, P * t : P * (t + 1)],
+                rhs=xw[:].bitcast(FP8X4),
+                rhs_scale=xs[:],
+                start=True,
+                stop=True,
+            )
+            nc.vector.tensor_scalar(
+                out=y[t][:, :S], in0=y_ps[:], scalar1=1.0, scalar2=None, op0=ALU.mult, op1=ALU.max, accum_out=top[t][:]
+            )
+            nc.vector.tensor_scalar(
+                out=bias[t][:], in0=top[t][:], scalar1=tau_t[:, t : t + 1], scalar2=-1.0, op0=ALU.mult, op1=ALU.mult
+            )
+            if t < last:
+                exp_gather(t, 0, S)
+            else:
+                exp_gather(t, 0, HALF)
+                exp_gather(t, HALF, S)
+        for t in range(PACK):
+            nc.vector.tensor_scalar(
+                out=yg[:, t, :], in0=y[t][:, :S], scalar1=gn_t[:, t : t + 1], scalar2=2.0, op0=ALU.mult, op1=ALU.mult
+            )
+
+        h = [keep.tile([P, S], F32, name=f"h{m}") for m in range(N // P)]
+
+        def second_product(h_ps, m, zq, zs):
+            nc.tensor.matmul_mx(
+                h_ps,
+                lhsT=w2[:, 2 * P * m : 2 * P * (m + 1)].bitcast(FP4X4),
+                lhsT_scale=w2s[:, P * m : P * (m + 1)],
+                rhs=zq[:].bitcast(FP8X4),
+                rhs_scale=zs[:],
+                start=True,
+                stop=True,
+            )
+
+        zq_half = []
+        for u in range(2):
+            z = keep.tile([P, HALF * PACK], BF16, name=f"z{u}", align_bytes=64)
+            zq = keep.tile([P, HALF], U32, name=f"zq{u}", align_bytes=64)
+            zs = keep.tile([P, HALF], U8, name=f"zs{u}", align_bytes=64)
+            cols = slice(u * HALF, (u + 1) * HALF)
+            nc.vector.tensor_tensor(
+                out=z[:].rearrange("p (c i t) -> p c t i", i=4, t=PACK),
+                in0=yg[:, :, cols].rearrange("p t (c i) -> p c t i", i=4),
+                in1=ea[:, :, cols].rearrange("p t (c i) -> p c t i", i=4),
+                op=ALU.mult,
+            )
+            nc.vector.quantize_mx(out=zq[:].bitcast(FP8X4), scales=zs[:], in_=z[:])
+            zq_half.append((zq, zs))
+
+        for m in range(N // P):
+            if m == 0:
+                for u in range(2):
+                    h_ps = psum.tile([P, HALF], F32, name=f"h_ps0_{u}", tag=f"bank{PACK + u}")
+                    second_product(h_ps[:], m, *zq_half[u])
+                    if u == 0:
+                        nc.scalar.copy(h[m][:, :HALF], h_ps[:])
+                    else:
+                        nc.vector.tensor_copy(h[m][:, HALF:], h_ps[:])
+            else:
+                h_ps = psum.tile([P, S], F32, name=f"h_ps{m}", tag=f"bank{m}")
+                for u in range(2):
+                    second_product(h_ps[:, u * HALF : (u + 1) * HALF], m, *zq_half[u])
+                nc.vector.tensor_copy(h[m][:], h_ps[:])
+
+        ra, rb = [], []
+        for m in range(N // P):
+            pa = keep.tile([P, W], F32, name=f"pa{m}")
+            pb = keep.tile([P, W], F32, name=f"pb{m}")
+            larger = keep.tile([P, W], F32, name=f"ra{m}")
+            smaller = keep.tile([P, W], F32, name=f"rb{m}")
+            nc.scalar.activation(out=pa[:], in_=h[m][:].indirect(n2_t[:]), func=ACT.Copy)
+            nc.scalar.activation(out=pb[:], in_=h[m][:].indirect(n3_t[:]), func=ACT.Copy)
+            nc.vector.tensor_tensor(out=larger[:], in0=pa[:], in1=pb[:], op=ALU.max)
+            nc.vector.tensor_tensor(out=smaller[:], in0=pa[:], in1=pb[:], op=ALU.min)
+            ra.append(larger)
+            rb.append(smaller)
+
+        def finish(m, pieces):
+            width = S // pieces
+            for k in range(pieces):
+                other = keep.tile([P, width], F32, name=f"other{m}_{k}")
+                res = keep.tile([P, width], F32, name=f"res{m}_{k}")
+                lo = k * width
+                nc.scalar.activation(
+                    out=other[:],
+                    in_=dt[m][:].indirect(n4_t[:, lo // LIST_ROWS : (lo + width) // LIST_ROWS]),
+                    func=ACT.Copy,
+                )
+                nc.vector.tensor_tensor(out=res[:], in0=dt[m][:, lo : lo + width], in1=other[:], op=ALU.subtract)
+                nc.sync.dma_start(out[P * m : P * (m + 1), lo : lo + width], res[:])
+
+        for m in range(N // P):
+            nc.scalar.activation(out=dt[m][:].indirect(n2_t[:]), in_=ra[m][:], func=ACT.Copy)
+            if m > 0:
+                finish(m - 1, 1)
+            nc.scalar.activation(out=dt[m][:].indirect(n3_t[:]), in_=rb[m][:], func=ACT.Copy)
+        finish(N // P - 1, 2)

@@ -219,7 +219,8 @@ def tile_picked_hashepkordd_none_p_kernel(
 
         for m in range(N // P):
             nc.scalar.activation(out=dt[m][:].indirect(n2_t[:]), in_=ra[m][:], func=ACT.Copy)
-            if m > 0:
-                finish(m - 1, 1)
+            if m > 1:
+                finish(m - 2, 1)
             nc.scalar.activation(out=dt[m][:].indirect(n3_t[:]), in_=rb[m][:], func=ACT.Copy)
+        finish(N // P - 2, 1)
         finish(N // P - 1, 2)

@@ -75,8 +75,8 @@ def tile_picked_hashepkordd_none_p_kernel(
         nc.sync.dma_start(xw_all[:].bitcast(I32), x_words[0].rearrange("p n t -> p (n t)").bitcast(I32))
         nc.scalar.dma_start(w1_raw[:].bitcast(I32), w1_words[0].bitcast(I32))
         nc.sync.dma_start(n1_t[:], n1)
-        nc.gpsimd.dma_start(tau_t[:], tau.rearrange("(p t) o -> p (t o)", t=PACK))
-        nc.gpsimd.dma_start(gn_t[:], gn.rearrange("(p t) o -> p (t o)", t=PACK))
+        nc.sync.dma_start(tau_t[:], tau.rearrange("(p t) o -> p (t o)", t=PACK))
+        nc.sync.dma_start(gn_t[:], gn.rearrange("(p t) o -> p (t o)", t=PACK))
 
         nc.vector.tensor_copy(xs_picked[:], xs_all[:].indirect(offs_t[:]))
         for s in range(PACK):

from contextlib import ExitStack

import concourse.mybir as mybir

K, T, S, H, N, W = 512, 2048, 256, 512, 512, 128
FLOPS = 2 * K * H * S + 2 * H * N * S

F32 = mybir.dt.float32
BF16 = mybir.dt.bfloat16
I32 = mybir.dt.int32
U32 = mybir.dt.uint32
U16 = mybir.dt.uint16
U8 = mybir.dt.uint8
FP8X4 = mybir.dt.float8_e4m3fn_x4
FP4X4 = mybir.dt.float4_e2m1fn_x4
ALU = mybir.AluOpType
ACT = mybir.ActivationFunctionType

P = 128
PACK = 4
QUAD = 32
SUB = 8
LIST_ROWS = 16
HALF = S // 2
SPARE = 16


def tile_picked_hashepkordd_none_p_kernel(
    tc, x_words, x_scales, w1_words, w1_scales, tau, gn, w2_words, w2_scales, offs, n1, n2, n3, n4, out
):
    nc = tc.nc
    with ExitStack() as ctx:
        keep = ctx.enter_context(tc.tile_pool(name="keep", bufs=1))
        psum = ctx.enter_context(tc.psum_pool(name="psum", bufs=1))

        offs_t = keep.tile([P, S // LIST_ROWS], U16, name="offs_t")
        n1_t = keep.tile([P, S // LIST_ROWS], U16, name="n1_t")
        n2_t = keep.tile([P, W // LIST_ROWS], U16, name="n2_t")
        n3_t = keep.tile([P, W // LIST_ROWS], U16, name="n3_t")
        n4_t = keep.tile([P, S // LIST_ROWS], U16, name="n4_t")

        xw_all = keep.tile([P, T], U32, name="xw_all", align_bytes=64)
        xs_all = keep.tile([P, T], U8, name="xs_all", align_bytes=64)
        xw = keep.tile([P, S], U32, name="xw", align_bytes=64)
        xs_picked = keep.tile([P, S], U8, name="xs_picked", align_bytes=64)
        xs = keep.tile([P, S], U8, name="xs", align_bytes=64)
        w1_raw = keep.tile([P, 2 * H], U8, name="w1_raw", align_bytes=64)
        w1s_raw = keep.tile([P, H], U8, name="w1s_raw", align_bytes=64)
        w1 = keep.tile([P, 2 * H], U8, name="w1", align_bytes=64)
        w1s = keep.tile([P, H], U8, name="w1s", align_bytes=64)
        w2 = w1_raw
        w2s = w1s_raw
        tau_t = keep.tile([P, PACK], F32, name="tau_t")
        gn_t = keep.tile([P, PACK], F32, name="gn_t")
        dt = [keep.tile([P, S + SPARE], F32, name=f"dt{m}") for m in range(N // P)]

        nc.vector.memset(xs[:].bitcast(I32), 0)
        for m in range(N // P):
            nc.vector.memset(dt[m][:, S:], 0.0)

        def load_w1_scales(queue, q):
            queue.dma_start(
                w1s_raw[QUAD * q : QUAD * (q + 1), :].bitcast(I32),
                w1_scales[0, PACK * q : PACK * q + PACK, :].bitcast(I32).partition_broadcast(SUB),
            )

        nc.sync.dma_start(offs_t[:], offs)
        nc.scalar.dma_start(
            xs_all[:].bitcast(I32), x_scales[0].bitcast(I32).unsqueeze(1).to_broadcast([LIST_ROWS, SUB, T // 4])
        )
        load_w1_scales(nc.sync, 0)
        load_w1_scales(nc.scalar, 1)
        load_w1_scales(nc.sync, 2)
        load_w1_scales(nc.scalar, 3)
        nc.sync.dma_start(xw_all[:].bitcast(I32), x_words[0].rearrange("p n t -> p (n t)").bitcast(I32))
        nc.scalar.dma_start(w1_raw[:].bitcast(I32), w1_words[0].bitcast(I32))
        nc.sync.dma_start(n1_t[:], n1)
        nc.sync.dma_start(tau_t[:], tau.rearrange("(p t) o -> p (t o)", t=PACK))
        nc.sync.dma_start(gn_t[:], gn.rearrange("(p t) o -> p (t o)", t=PACK))

        nc.vector.tensor_copy(xs_picked[:], xs_all[:].indirect(offs_t[:]))
        for s in range(PACK):
            nc.scalar.dma_start(xs[s:P:QUAD, :].bitcast(I32), xs_picked[SUB * s : P : QUAD, :].bitcast(I32))

        nc.scalar.copy(
            w1[:].bitcast(U16).rearrange("p (t m) -> p t m", t=PACK),
            w1_raw[:].bitcast(U16).rearrange("p (m t) -> p t m", t=PACK),
        )
        nc.vector.tensor_copy(
            w1s[:].rearrange("p (t m) -> p t m", t=PACK),
            w1s_raw[:].rearrange("p (m t) -> p t m", t=PACK),
        )
        nc.vector.tensor_copy(xw[:], xw_all[:].indirect(offs_t[:]))

        nc.sync.dma_start(w2[:].bitcast(I32), w2_words[0].bitcast(I32))
        nc.sync.dma_start(n2_t[:], n2)
        nc.sync.dma_start(n3_t[:], n3)
        nc.sync.dma_start(n4_t[:], n4)
        for q in range(P // QUAD):
            nc.sync.dma_start(
                w2s[QUAD * q : QUAD * q + PACK, :].bitcast(I32),
                w2_scales[0, PACK * q : PACK * q + PACK, :].bitcast(I32),
            )

        last = PACK - 1
        y = [keep.tile([P, S if t == last else 2 * S], F32, name=f"y{t}") for t in range(PACK)]
        for t in range(last):
            nc.vector.memset(y[t][:, S:], 0.0)
        top = [keep.tile([P, 1], F32, name=f"top{t}") for t in range(PACK)]
        bias = [keep.tile([P, 1], F32, name=f"bias{t}") for t in range(PACK)]
        yg = keep.tile([P, PACK, S], F32, name="yg")
        ea = keep.tile([P, PACK, S], F32, name="ea")

        def exp_gather(t, lo, hi):
            nc.scalar.activation(
                out=ea[:, t, lo:hi],
                in_=y[t][:].indirect(n1_t[:, lo // LIST_ROWS : hi // LIST_ROWS]),
                func=ACT.Exp,
                scale=tau_t[:, t : t + 1],
                bias=bias[t][:],
            )

        for t in range(PACK):
            y_ps = psum.tile([P, S], F32, name=f"y_ps{t}", tag=f"bank{t}")
            nc.tensor.matmul_mx(
                y_ps[:],
                lhsT=w1[:, 2 * P * t : 2 * P * (t + 1)].bitcast(FP4X4),
                lhsT_scale=w1s[:, P * t : P * (t + 1)],
                rhs=xw[:].bitcast(FP8X4),
                rhs_scale=xs[:],
                start=True,
                stop=True,
            )
            nc.vector.tensor_scalar(
                out=y[t][:, :S], in0=y_ps[:], scalar1=1.0, scalar2=None, op0=ALU.mult, op1=ALU.max, accum_out=top[t][:]
            )
            nc.vector.tensor_scalar(
                out=bias[t][:], in0=top[t][:], scalar1=tau_t[:, t : t + 1], scalar2=-1.0, op0=ALU.mult, op1=ALU.mult
            )
            if t < last:
                exp_gather(t, 0, S)
            else:
                exp_gather(t, 0, HALF)
                exp_gather(t, HALF, S)
        for t in range(PACK):
            nc.vector.tensor_scalar(
                out=yg[:, t, :], in0=y[t][:, :S], scalar1=gn_t[:, t : t + 1], scalar2=2.0, op0=ALU.mult, op1=ALU.mult
            )

        h = [keep.tile([P, S], F32, name=f"h{m}") for m in range(N // P)]

        def second_product(h_ps, m, zq, zs):
            nc.tensor.matmul_mx(
                h_ps,
                lhsT=w2[:, 2 * P * m : 2 * P * (m + 1)].bitcast(FP4X4),
                lhsT_scale=w2s[:, P * m : P * (m + 1)],
                rhs=zq[:].bitcast(FP8X4),
                rhs_scale=zs[:],
                start=True,
                stop=True,
            )

        zq_half = []
        for u in range(2):
            z = keep.tile([P, HALF * PACK], BF16, name=f"z{u}", align_bytes=64)
            zq = keep.tile([P, HALF], U32, name=f"zq{u}", align_bytes=64)
            zs = keep.tile([P, HALF], U8, name=f"zs{u}", align_bytes=64)
            cols = slice(u * HALF, (u + 1) * HALF)
            nc.vector.tensor_tensor(
                out=z[:].rearrange("p (c i t) -> p c t i", i=4, t=PACK),
                in0=yg[:, :, cols].rearrange("p t (c i) -> p c t i", i=4),
                in1=ea[:, :, cols].rearrange("p t (c i) -> p c t i", i=4),
                op=ALU.mult,
            )
            nc.vector.quantize_mx(out=zq[:].bitcast(FP8X4), scales=zs[:], in_=z[:])
            zq_half.append((zq, zs))

        for m in range(N // P):
            if m == 0:
                for u in range(2):
                    h_ps = psum.tile([P, HALF], F32, name=f"h_ps0_{u}", tag=f"bank{PACK + u}")
                    second_product(h_ps[:], m, *zq_half[u])
                    if u == 0:
                        nc.scalar.copy(h[m][:, :HALF], h_ps[:])
                    else:
                        nc.vector.tensor_copy(h[m][:, HALF:], h_ps[:])
            else:
                h_ps = psum.tile([P, S], F32, name=f"h_ps{m}", tag=f"bank{m}")
                for u in range(2):
                    second_product(h_ps[:, u * HALF : (u + 1) * HALF], m, *zq_half[u])
                nc.vector.tensor_copy(h[m][:], h_ps[:])

        ra, rb = [], []
        for m in range(N // P):
            pa = keep.tile([P, W], F32, name=f"pa{m}")
            pb = keep.tile([P, W], F32, name=f"pb{m}")
            larger = keep.tile([P, W], F32, name=f"ra{m}")
            smaller = keep.tile([P, W], F32, name=f"rb{m}")
            nc.scalar.activation(out=pa[:], in_=h[m][:].indirect(n2_t[:]), func=ACT.Copy)
            nc.scalar.activation(out=pb[:], in_=h[m][:].indirect(n3_t[:]), func=ACT.Copy)
            nc.vector.tensor_tensor(out=larger[:], in0=pa[:], in1=pb[:], op=ALU.max)
            nc.vector.tensor_tensor(out=smaller[:], in0=pa[:], in1=pb[:], op=ALU.min)
            ra.append(larger)
            rb.append(smaller)

        def finish(m, pieces):
            width = S // pieces
            for k in range(pieces):
                other = keep.tile([P, width], F32, name=f"other{m}_{k}")
                res = keep.tile([P, width], F32, name=f"res{m}_{k}")
                lo = k * width
                nc.scalar.activation(
                    out=other[:],
                    in_=dt[m][:].indirect(n4_t[:, lo // LIST_ROWS : (lo + width) // LIST_ROWS]),
                    func=ACT.Copy,
                )
                nc.vector.tensor_tensor(out=res[:], in0=dt[m][:, lo : lo + width], in1=other[:], op=ALU.subtract)
                nc.sync.dma_start(out[P * m : P * (m + 1), lo : lo + width], res[:])

        for m in range(N // P):
            nc.scalar.activation(out=dt[m][:].indirect(n2_t[:]), in_=ra[m][:], func=ACT.Copy)
            if m > 1:
                finish(m - 2, 1)
            nc.scalar.activation(out=dt[m][:].indirect(n3_t[:]), in_=rb[m][:], func=ACT.Copy)
        finish(N // P - 2, 1)
        finish(N // P - 1, 2)
